import numpy as np
import ml_dtypes


def mxq(x, axis, fmt="e4m3"):
    dtype, down = {"e4m3": (ml_dtypes.float8_e4m3fn, 7), "e5m2": (ml_dtypes.float8_e5m2, 14)}[fmt]
    v = np.moveaxis(np.asarray(x, np.float32).astype(ml_dtypes.bfloat16).astype(np.float64), axis, -1)
    blocks = v.reshape(v.shape[:-1] + (-1, 32))
    amax = np.abs(blocks).max(-1, keepdims=True)
    byte = np.maximum(np.where(amax > 0, np.frexp(amax)[1] - 1 + 127, 0) - down, 1)
    scale = np.exp2(byte - 127.0)
    codes = (blocks / scale).astype(np.float32).astype(dtype).astype(np.float64)
    return np.moveaxis((codes * scale).reshape(v.shape), -1, axis)


WIDE = False


def mx_kscale(k):
    if not WIDE:
        return np.ones(k)
    levels = np.array([10, -10, 5, -5, 0])
    if k % 512:
        return np.exp2(np.random.permutation(np.resize(levels, k // 32))).repeat(32)
    a = np.empty((k // 512, 16))
    for p in range(k // 512):
        a[p, :8] = np.random.permutation(np.resize(levels, 8))
        for g in range(8):
            far = levels[np.abs(levels - a[p, g]) >= 10]
            a[p, g + 8] = far[np.random.randint(len(far))]
    return np.exp2(a.ravel()).repeat(32)


BF16 = ml_dtypes.bfloat16


def bf(x):
    return np.asarray(x, np.float32).astype(BF16)


def f64(x):
    return np.asarray(x).astype(np.float64)


E2M1 = np.array([0.0, 0.5, 1.0, 1.5, 2.0, 3.0, 4.0, 6.0, -0.0, -0.5, -1.0, -1.5, -2.0, -3.0, -4.0, -6.0])


def pack_weight(w, fmt):
    k, n = w.shape
    w = f64(bf(w)).reshape(k // 32, 32, n)
    amax = np.abs(w).max(1)
    if fmt == "e4m3":
        byte = np.frexp(amax)[1] - 1 + 127 - 7
    else:
        mant, ex = np.frexp(amax / 6.0)
        byte = np.where(mant > 0.5, ex, ex - 1) + 127
    byte = np.clip(np.where(amax > 0, byte, 1), 1, 254)
    scaled = (w * np.exp2(127.0 - byte)[:, None, :]).reshape(k, n).astype(np.float32)
    by_word = np.ascontiguousarray(scaled.reshape(k // 512, 128, 4, n).transpose(0, 1, 3, 2))
    if fmt == "e4m3":
        words = by_word.astype(ml_dtypes.float8_e4m3fn).view(np.uint8)
    else:
        c = by_word.astype(ml_dtypes.float4_e2m1fn).view(np.uint8) & 0xF
        words = c[..., 0::2] | (c[..., 1::2] << 4)
    return np.ascontiguousarray(words), np.ascontiguousarray(byte.astype(np.uint8).reshape(k // 512, 16, n))


def unpack_weight(words, scales, fmt):
    g, p, n, _ = words.shape
    if fmt == "e4m3":
        vals = np.ascontiguousarray(words).view(ml_dtypes.float8_e4m3fn).astype(np.float64)
    else:
        nib = np.empty((g, p, n, 4), np.uint8)
        nib[..., 0::2] = words & 0xF
        nib[..., 1::2] = words >> 4
        vals = E2M1[nib]
    vals = vals * np.repeat(np.exp2(scales.astype(np.float64) - 127.0), 8, axis=1)[..., None]
    return vals.transpose(0, 1, 3, 2).reshape(g * 512, n)
def pack4(w):
    words, scales = pack_weight(w, "e2m1")
    return words.reshape(words.shape[0], 128, -1), scales


def unpack4(words, scales):
    return unpack_weight(words.reshape(words.shape[0], 128, -1, 2), scales, "e2m1")


D, K, V, NQ, R = 1024, 1024, 2048, 512, 512
SPREAD = 1.8
PRIOR = 0.3


def setup_inputs():
    s, t, u = mx_kscale(K), mx_kscale(V), mx_kscale(D)
    theta = np.exp(SPREAD * np.random.standard_normal((D, K)) - SPREAD ** 2 / 2)
    phi = np.exp(SPREAD * np.random.standard_normal((K, V)) - SPREAD ** 2 / 2) / K
    imp = np.random.uniform(0.5, 1.5, (D, V))
    query = np.random.standard_normal((V, NQ)) / np.sqrt(V)
    query_words, query_scales = pack4(query / t[:, None])
    return {"theta": bf(theta * s),
            "phi": bf(phi / s[:, None]),
            "back": bf(PRIOR * np.random.uniform(0.5, 1.5, V)),
            "imp": bf(imp * u[:, None] * t),
            "query_words": query_words,
            "query_scales": query_scales,
            "fb": bf(np.random.standard_normal((R, D)) / np.sqrt(D) / u)}


def reference(theta, phi, back, imp, query_words, query_scales, fb):
    h = mxq(f64(theta), 1, "e4m3") @ mxq(f64(phi), 0, "e4m3")
    logp = np.log(h + f64(back)) * f64(imp)
    y = unpack4(query_words, query_scales)
    scores = mxq(logp, 1, "e4m3") @ y
    profiles = mxq(f64(fb), 1, "e4m3") @ mxq(logp, 0, "e4m3")
    return scores, profiles

from contextlib import ExitStack

import concourse.mybir as mybir
from concourse.masks import make_identity

F32 = mybir.dt.float32
BF16 = mybir.dt.bfloat16
I32 = mybir.dt.int32
U32 = mybir.dt.uint32
U8 = mybir.dt.uint8
E4M3 = mybir.dt.float8_e4m3fn_x4
E2M1 = mybir.dt.float4_e2m1fn_x4
LN = mybir.ActivationFunctionType.Ln
MULT = mybir.AluOpType.mult
ADD = mybir.AluOpType.add

P = 128
D, K, V, NQ, R = 1024, 1024, 2048, 512, 512
FLOPS = 2 * (D * K * V + D * V * NQ + R * D * V)

ORDER = [(0, 0), (1, 0), (0, 1), (0, 2), (0, 3), (1, 1), (1, 2), (1, 3)]


def tile_weighted_log_frequency_search_s8_kernel(tc, theta, phi, back, imp, query_words, query_scales, fb, out_0, out_1):
    nc = tc.nc
    with ExitStack() as ctx:
        keep = ctx.enter_context(tc.tile_pool(name="keep", bufs=1))
        work = ctx.enter_context(tc.tile_pool(name="work", bufs=2))
        psum = ctx.enter_context(tc.psum_pool(name="psum", bufs=2))
        ctx.enter_context(tc.manual_schedule())

        theta_raw = [keep.tile([P, 4, K], BF16, name="theta_raw%d" % g, tag="rows", bufs=2, align_bytes=64) for g in range(2)]
        theta_codes = [keep.tile([P, 2, 512], U32, name="theta_codes%d" % g, align_bytes=64) for g in range(2)]
        theta_scales = [keep.tile([P, 2, 512], U8, name="theta_scales%d" % g, align_bytes=64) for g in range(2)]
        phi_raw = {(g, c): keep.tile([P, 4, 512], BF16, name="phi_raw%d%d" % (g, c), align_bytes=64) for g in range(4) for c in range(2)}
        phi_codes = [keep.tile([P, 2, 512], U32, name="phi_codes%d" % g, align_bytes=64) for g in range(4)]
        phi_scales = [keep.tile([P, 2, 512], U8, name="phi_scales%d" % g, align_bytes=64) for g in range(4)]
        imp_raw = {}
        fb_raw = keep.tile([P, 4, D], BF16, name="fb_raw", tag="rows", bufs=2, align_bytes=64)
        fb_codes = keep.tile([P, 2, R], U32, name="fb_codes", align_bytes=64)
        fb_scales = keep.tile([P, 2, R], U8, name="fb_scales", align_bytes=64)
        q_words = keep.tile([P, 4, 2 * NQ], U8, name="q_words", align_bytes=64)
        q_scales = keep.tile([P, 4, NQ], U8, name="q_scales", align_bytes=64)
        back_sb = keep.tile([P, 4, 4], BF16, name="back_sb", align_bytes=64)
        v_codes = [keep.tile([P, 4, 512], U32, name="v_codes%d" % g, align_bytes=64) for g in range(2)]
        v_scales = [keep.tile([P, 4, 512], U8, name="v_scales%d" % g, align_bytes=64) for g in range(2)]
        d_codes = [keep.tile([P, 2, 512], U32, name="d_codes%d" % g, align_bytes=64) for g in range(4)]
        d_scales = [keep.tile([P, 2, 512], U8, name="d_scales%d" % g, align_bytes=64) for g in range(4)]
        ident = keep.tile([P, P], F32, name="ident", align_bytes=64)
        dummy = keep.tile([P, 1], F32, name="dummy", align_bytes=64)

        theta_rows = theta.rearrange("(g m t) k -> g m t k", g=2, m=P)
        phi_rows = phi.rearrange("(c p j) v -> c p j v", c=2, p=P)
        imp_rows = imp.rearrange("(g m t) v -> g m t v", g=2, m=P)

        def load_theta(g):
            for a in range(2):
                nc.sync.dma_start(out=theta_raw[g][:, 2 * a : 2 * a + 2, :], in_=theta_rows[g][:, 2 * a : 2 * a + 2, :])

        def load_phi(g):
            for c in range(2):
                nc.sync.dma_start(out=phi_raw[g, c][:], in_=phi_rows[c][:, :, 512 * g : 512 * (g + 1)])

        def load_imp(g, c):
            imp_raw[g, c] = keep.tile([P, 4, 1024], BF16, name="imp_raw", tag="imp", bufs=3, align_bytes=64)
            nc.sync.dma_start(out=imp_raw[g, c][:], in_=imp_rows[g][:, :, 1024 * c : 1024 * (c + 1)])

        load_theta(0)
        load_phi(0)
        nc.scalar.dma_start(out=back_sb[:], in_=back.rearrange("(g p t) -> p g t", g=4, p=P))
        load_imp(0, 0)
        load_theta(1)
        load_imp(1, 0)
        load_phi(1)
        load_phi(2)
        make_identity(nc, ident[:])
        nc.gpsimd.memset(q_scales[:].bitcast(U32), 0)
        nc.vector.memset(dummy[:], 1.0)
        nc.scalar.activation(out=dummy[:], in_=dummy[:], func=LN)

        def load_late():
            nc.sync.dma_start(out=fb_raw[:], in_=fb.rearrange("(c r) d -> r c d", r=P))
            load_phi(3)
            load_imp(0, 1)
            nc.sync.dma_start(out=q_words[:].bitcast(I32), in_=query_words.rearrange("g p n -> p g n").bitcast(I32))
            for q in range(4):
                nc.sync.dma_start(
                    out=q_scales[32 * q : 32 * q + 4].bitcast(I32),
                    in_=query_scales.rearrange("g q n -> q g n")[4 * q : 4 * q + 4].bitcast(I32),
                )

        def copy(eng, out, in_):
            if eng == "s":
                nc.scalar.copy(out=out, in_=in_)
            elif eng == "g":
                nc.gpsimd.tensor_scalar(out=out, in0=in_, scalar1=1.0, scalar2=0.0, op0=MULT, op1=ADD)
            else:
                nc.vector.tensor_copy(out=out, in_=in_)

        def quantize(codes, scales, grouped):
            nc.vector.quantize_mx(out=codes.bitcast(E4M3), scales=scales, in_=grouped.rearrange("p c t -> p (c t)"))

        theta_grouped = {}

        def theta_turn(g, a, c, eng, tag):
            if (g, c) not in theta_grouped:
                theta_grouped[g, c] = work.tile([P, 512, 4], BF16, name="theta_grouped", tag="theta_grouped", bufs=2, align_bytes=64)
            bank = psum.tile([P, 2, 2, P], F32, name=tag, tag=tag, bufs=2)
            words = theta_raw[g][:].bitcast(F32)
            for e in range(2):
                for u in range(2):
                    nc.tensor.transpose(bank[:, e, u, :], words[:, 2 * a + e, 256 * c + u : 256 * (c + 1) : 2], ident[:])
            copy(
                eng,
                theta_grouped[g, c][:].bitcast(F32)[:, 256 * a : 256 * (a + 1), :].rearrange("p (m e) u -> p m e u", e=2),
                bank[:].rearrange("p e u m -> p m e u"),
            )

        def theta_quantize(g, c):
            quantize(theta_codes[g][:, c, :], theta_scales[g][:, c, :], theta_grouped[g, c][:])

        phi_grouped = {}

        def phi_interleave(g, c, half, eng):
            if (g, c) not in phi_grouped:
                phi_grouped[g, c] = work.tile([P, 512, 4], BF16, name="phi_grouped", tag="phi_grouped", bufs=3, align_bytes=64)
            copy(
                eng,
                phi_grouped[g, c][:, 256 * half : 256 * (half + 1), :].rearrange("p (t m) j -> p t m j", t=2),
                phi_raw[g, c][:].rearrange("p j (m h t) -> p h t m j", h=2, t=2)[:, half],
            )

        def phi_quantize(g, c, half=None):
            cols = slice(0, 512) if half is None else slice(256 * half, 256 * (half + 1))
            quantize(phi_codes[g][:, c, cols], phi_scales[g][:, c, cols], phi_grouped[g, c][:, cols, :])

        fb_grouped = {}

        def fb_turn(g, b, eng, tag):
            if g not in fb_grouped:
                fb_grouped[g] = work.tile([P, R, 4], BF16, name="fb_grouped", tag="theta_grouped", bufs=2, align_bytes=64)
            bank = psum.tile([P, 2, 2, P], F32, name=tag, tag=tag, bufs=2)
            words = fb_raw[:].bitcast(F32)
            for c in range(2):
                for u in range(2):
                    nc.tensor.transpose(bank[:, c, u, :], words[:, 2 * b + c, 256 * g + u : 256 * (g + 1) : 2], ident[:])
            copy(
                eng,
                fb_grouped[g][:].bitcast(F32)[:, 256 * b : 256 * (b + 1), :].rearrange("p (c r) u -> p c r u", c=2),
                bank[:].rearrange("p c u r -> p c r u"),
            )

        def fb_quantize(g):
            quantize(fb_codes[:, g, :], fb_scales[:, g, :], fb_grouped[g][:])

        imp_bank, h_bank, x_tile, l_tile, lt_bank, v_grouped, d_grouped = {}, {}, {}, {}, {}, {}, {}

        def imp_turn(h):
            n, s = divmod(h, 2)
            g, w = ORDER[n]
            imp_bank[h] = psum.tile([P, 4, P], F32, name="it", tag="it", bufs=2)
            words = imp_raw[g, w // 2][:].bitcast(F32)
            first = 256 * (w % 2) + s
            for t in range(4):
                nc.tensor.transpose(imp_bank[h][:, t, :], words[:, t, first : 256 * (w % 2 + 1) : 2], ident[:])

        def freq(h, e):
            n, s = divmod(h, 2)
            g, w = ORDER[n]
            t = 2 * s + e
            bank = psum.tile([P, 512], F32, name="h", tag="h", bufs=2)
            h_bank[h, e] = bank
            for c in range(2):
                nc.tensor.matmul_mx(
                    out=bank[:],
                    lhsT=phi_codes[w][:, c, P * t : P * (t + 1)].bitcast(E4M3),
                    lhsT_scale=phi_scales[w][:, c, P * t : P * (t + 1)],
                    rhs=theta_codes[g][:, c, :].bitcast(E4M3),
                    rhs_scale=theta_scales[g][:, c, :],
                    start=(c == 0),
                    stop=(c == 1),
                )

        def log(h, e):
            n, s = divmod(h, 2)
            g, w = ORDER[n]
            t = 2 * s + e
            if e == 0:
                x_tile[h] = work.tile([P, 2, 512], F32, name="x", tag="x", bufs=3, align_bytes=64)
            nc.scalar.activation(out=x_tile[h][:, e, :], in_=h_bank[h, e][:], func=LN, bias=back_sb[:, w, t : t + 1])

        def weigh(h, e):
            n, s = divmod(h, 2)
            if n not in l_tile:
                l_tile[n] = work.tile([P, 4, 512], BF16, name="l", tag="l", bufs=3, align_bytes=64)
            nc.vector.tensor_tensor(
                out=l_tile[n][:, 2 * s + e, :].rearrange("p (a m e) -> p a m e", a=2, e=2),
                in0=x_tile[h][:, e, :].rearrange("p (a m e) -> p a m e", a=2, e=2),
                in1=imp_bank[h][:].bitcast(BF16).rearrange("p (a e) (m s) -> p a m e s", a=2, s=2)[:, :, :, :, e],
                op=MULT,
            )

        def l_turn(h):
            n, s = divmod(h, 2)
            lt_bank[h] = psum.tile([P, 2, 2, P], F32, name="lt", tag="lt", bufs=2)
            for e in range(2):
                words = l_tile[n][:, 2 * s + e, :].bitcast(F32)
                for a in range(2):
                    nc.tensor.transpose(lt_bank[h][:, e, a, :], words[:, P * a : P * (a + 1)], ident[:])

        def l_turn_copy(h, eng):
            n, s = divmod(h, 2)
            if n not in d_grouped:
                d_grouped[n] = work.tile([P, 512, 4], BF16, name="d_grouped", tag="d_grouped", bufs=2, align_bytes=64)
            copy(
                eng,
                d_grouped[n][:].bitcast(F32).rearrange("m (p u e) a -> m u p e a", u=2, e=2)[:, s],
                lt_bank[h][:].rearrange("m e a p -> m p e a"),
            )

        def v_interleave(n, a, eng):
            if n not in v_grouped:
                v_grouped[n] = work.tile([P, 512, 4], BF16, name="v_grouped", tag="v_grouped", bufs=2, align_bytes=64)
            copy(
                eng,
                v_grouped[n][:].rearrange("p (m a e) t -> p a m e t", a=2, e=2)[:, a],
                l_tile[n][:].rearrange("p t (a m e) -> p a m e t", a=2, e=2)[:, a],
            )

        def v_quantize(n):
            g, w = ORDER[n]
            quantize(v_codes[g][:, w, :], v_scales[g][:, w, :], v_grouped[n][:])

        def d_quantize(n):
            g, w = ORDER[n]
            quantize(d_codes[w][:, g, :], d_scales[w][:, g, :], d_grouped[n][:])

        out_bank = {}

        def score_pass(g, j, w, tag="o"):
            if w == 0:
                out_bank["s", g, j] = psum.tile([P, 512], F32, name=tag, tag=tag, bufs=2)
            nc.tensor.matmul_mx(
                out=out_bank["s", g, j][:],
                lhsT=v_codes[g][:, w, P * j : P * (j + 1)].bitcast(E4M3),
                lhsT_scale=v_scales[g][:, w, P * j : P * (j + 1)],
                rhs=q_words[:, w, :].bitcast(E2M1),
                rhs_scale=q_scales[:, w, :],
                start=(w == 0),
                stop=(w == 3),
            )

        def store(key, eng, dest):
            stage = work.tile([P, 512], F32, name="stage", tag="stage", bufs=8, align_bytes=64)
            copy(eng, stage[:], out_bank[key][:])
            nc.sync.dma_start(out=dest, in_=stage[:])

        def score_store(g, j, eng):
            row = 512 * g + P * j
            store(("s", g, j), eng, out_0[row : row + P, :])

        def score(g, j, eng):
            for w in range(4):
                score_pass(g, j, w)
            score_store(g, j, eng)

        def profile(w, c, eng, tag="o"):
            bank = psum.tile([P, 512], F32, name=tag, tag=tag, bufs=2)
            out_bank["p", w, c] = bank
            for g in range(2):
                nc.tensor.matmul_mx(
                    out=bank[:],
                    lhsT=fb_codes[:, g, P * c : P * (c + 1)].bitcast(E4M3),
                    lhsT_scale=fb_scales[:, g, P * c : P * (c + 1)],
                    rhs=d_codes[w][:, g, :].bitcast(E4M3),
                    rhs_scale=d_scales[w][:, g, :],
                    start=(g == 0),
                    stop=(g == 1),
                )
            store(("p", w, c), eng, out_1[P * c : P * (c + 1), 512 * w : 512 * (w + 1)])

        for a in range(2):
            theta_turn(0, a, 0, "s", "lt")
            theta_turn(0, a, 1, "v", "it")
        theta_quantize(0, 0)
        theta_quantize(0, 1)
        phi_interleave(0, 0, 0, "v")
        phi_interleave(0, 0, 1, "s")
        phi_interleave(0, 1, 0, "v")
        phi_quantize(0, 0, 0)
        phi_quantize(0, 1, 0)
        phi_interleave(0, 1, 1, "v")
        phi_quantize(0, 0, 1)
        phi_quantize(0, 1, 1)
        load_late()

        def products(h):
            if 7 <= h <= 10:
                profile(0, h - 7, "s")
            if 11 <= h <= 14:
                score(0, h - 11, "s")
            if h in (15, 16):
                profile(1, 2 * (h - 15), "s")
                profile(1, 2 * (h - 15) + 1, "v")
            if h == 17:
                for c in range(4):
                    profile(2, c, "s" if c % 2 else "v", "h" if c % 2 else "o")
                for j in range(4):
                    for w in range(3):
                        score_pass(1, j, w, "h" if j % 2 else "o")
            if h == 18:
                for j in range(4):
                    score_pass(1, j, 3)
                    score_store(1, j, "s" if j % 2 else "v")
                for c in range(4):
                    profile(3, c, "s" if c % 2 else "v", "h" if c % 2 else "o")

        for h in range(19):
            n, s = divmod(h, 2)
            if h == 0:
                for e in range(2):
                    freq(h, e)
                    log(h, e)
            if h < 16:
                imp_turn(h)
            if h == 5:
                load_imp(1, 1)
            if 0 <= h - 2 < 16:
                l_turn(h - 2)
                l_turn_copy(h - 2, "s")
            if 0 < h < 16:
                for e in range(2):
                    freq(h, e)
                    log(h, e)
            if 0 <= h - 1 < 16:
                weigh(h - 1, 0)
                weigh(h - 1, 1)
            if s == 0 and 0 <= n - 2 < 8:
                d_quantize(n - 2)
            if s == 0 and 0 <= n - 1 < 8:
                v_interleave(n - 1, 0, "v")
                v_interleave(n - 1, 1, "s" if n < 8 else "v")
            if s == 1 and 0 <= n - 1 < 8:
                v_quantize(n - 1)
            if h == 0:
                theta_turn(1, 0, 0, "s", "lt")
                theta_turn(1, 0, 1, "v", "lt")
            if h == 1:
                theta_turn(1, 1, 0, "s", "lt")
                theta_turn(1, 1, 1, "v", "lt")
                theta_quantize(1, 0)
                theta_quantize(1, 1)
            if h in (2, 4, 6):
                g = h // 2
                phi_interleave(g, 0, 0, "v")
                phi_interleave(g, 1, 0, "s")
                phi_interleave(g, 0, 1, "v")
            if h in (3, 5, 7):
                g = h // 2
                phi_interleave(g, 1, 1, "v")
                phi_quantize(g, 0)
                phi_quantize(g, 1)
            if h in (4, 5):
                fb_turn(h - 4, 0, "s", "lt")
                fb_turn(h - 4, 1, "v", "lt")
                fb_quantize(h - 4)
            products(h)
